import numpy as np, ml_dtypes
CORES = [4,12,20,28,44,60,76,84,92,108,116,124]
N = 12
TK = 64
def setup_inputs(rng):
    return {"x": rng.standard_normal((N, 128, TK), dtype=np.float32).astype(ml_dtypes.bfloat16), "w1": (rng.standard_normal((N, 128, 128), dtype=np.float32) / 8).astype(ml_dtypes.bfloat16), "w2": (rng.standard_normal((N, 128, 128), dtype=np.float32) / 8).astype(ml_dtypes.bfloat16)}
def setup_inputs_big(rng):
    d = setup_inputs(rng)
    for k in ("x", "w1", "w2"): d[k] = (d[k].astype(np.float32) * 1024.0).astype(d[k].dtype)
    return d
def setup_inputs_small(rng):
    d = setup_inputs(rng)
    for k in ("x", "w1", "w2"): d[k] = (d[k].astype(np.float32) * (1 / 1024.0)).astype(d[k].dtype)
    return d
def setup_inputs_apart(rng):
    d = setup_inputs(rng)
    f = (10.0 ** rng.permutation(np.linspace(-1.5, 1.5, N))).astype(np.float32).reshape(N, 1, 1)
    for k in ("x", "w1", "w2"): d[k] = (d[k].astype(np.float32) * f).astype(d[k].dtype)
    return d
def reference(x, w1, w2):
    X, W1, W2 = x.astype(np.float64), w1.astype(np.float64), w2.astype(np.float64)
    y = np.zeros((N, 128, TK))
    for r in range(N):
        for j in range(N):
            y[r] += W2[j].T @ np.maximum(W1[j].T @ X[r], 0.0)
    return {"y": y.astype(ml_dtypes.bfloat16 if x.dtype != np.float64 else np.float64)}

@@ -1,0 +1,159 @@
+from concourse.bass import DstId, RemoteDMATransfer
+from concourse.mybir import AluOpType
+
+N = 12
+TK = 64
+WW = 256
+BANKS = 4
+DIRECT = 3
+PER = 2
+
+SCRATCH = {
+    "W": ("sbuf", [128, N * WW], "bfloat16"),
+    "xs": ("sbuf", [128, TK], "bfloat16"),
+    "hs": ("sbuf", [128, N * TK], "bfloat16"),
+    "zero": ("sbuf", [128, TK], "float32"),
+    "ys": ("sbuf", [128, TK], "bfloat16"),
+    "yp": ("psum", [128, 512], "float32"),
+}
+for _b in range(BANKS):
+    SCRATCH["hp%d" % _b] = ("psum", [128, 512], "float32")
+
+SEMAPHORES = (["loaded", "xl", "fed", "sent", "z", "yd", "yc", "stored"]
+              + ["a%d" % _i for _i in range(N)]
+              + ["m%d" % _i for _i in range(N)]
+              + ["r%d" % _i for _i in range(N)])
+
+_CACHE = {}
+
+
+def _plan(cores, topo):
+    n = len(cores)
+    chips = [topo.chip(c) for c in cores]
+    every = range(topo.CHIPS * topo.CORES_PER_CHIP)
+    out = []
+    for s, R in enumerate(cores):
+        grp = [t for t in range(n) if t == s or topo.same_plane(chips[s], chips[t])]
+        oth = [t for t in range(n) if t not in grp]
+        i, g = grp.index(s), len(grp)
+        ring = [grp[(i + k) % g] for k in range(1, g)]
+        mine = [c for c in every if topo.chip(c) == chips[s] and c != R]
+        port = [c for c in mine if all(topo.may_write(c, cores[t]) for t in oth)]
+        near = ([c for c in port if topo.die(c) == topo.die(R)]
+                + [c for c in mine if c not in port and topo.die(c) == topo.die(R)])
+        far = ([c for c in port if topo.die(c) != topo.die(R)]
+               + [c for c in mine if c not in port and topo.die(c) != topo.die(R)])
+        direct, rest = ring[:DIRECT], ring[DIRECT:]
+        q = 2 * max(1, g // len(oth))
+        rot = [(k + i) % len(oth) for k in range(len(oth))]
+        nx = [oth[k] for k in rot if (i + k) % q == 0]
+        fx = [oth[k] for k in rot if (i + k) % q != 0]
+        fill = len(nx) % PER
+        helpers = []
+        for lst, cs in ((fx + rest[fill:], far), (nx + rest[:fill], near)):
+            for j in range(0, len(lst), PER):
+                helpers.append((cs[j // PER], lst[j:j + PER]))
+        for h, ts in helpers:
+            assert all(topo.may_write(h, cores[t]) for t in ts)
+        out.append({"direct": direct, "helpers": helpers})
+    return out
+
+
+def _bits(m):
+    return bin(m).count("1")
+
+
+def rank_program(g, core, T, topo):
+    cores = list(T.cores)
+    if "plan" not in _CACHE:
+        _CACHE["plan"] = _plan(cores, topo)
+    plan = _CACHE["plan"]
+    sem = T.sem
+
+    def slot(s):
+        return T.W[:, s * WW:(s + 1) * WW]
+
+    def common_mask(src, dsts):
+        m = topo.mask(src, dsts[0])
+        for d in dsts[1:]:
+            m &= topo.mask(src, d)
+        return m
+
+    def send(s, dsts, rsem):
+        m = common_mask(core, dsts)
+        ids = [DstId(rid=topo.addr(d)[0], pnc=topo.addr(d)[1]) for d in dsts]
+        g.remote_dma_fused([RemoteDMATransfer(dst_ids=ids, dma_engine_mask=m, remote_sem=rsem, srcs=[slot(s)],
+                                              dsts=[slot(s) for _ in dsts], alu_op=0)], local_sem=sem.sent)
+        return _bits(m)
+
+    rank = T.rank_of(core)
+    if rank is None:
+        for s, p in enumerate(plan):
+            for h, ts in p["helpers"]:
+                if h == core:
+                    g.wait_ge(sem.fed, _bits(common_mask(cores[s], [c for c, _ in p["helpers"]])))
+                    k = send(s, [cores[t] for t in ts], sem["a%d" % s])
+                    g.wait_ge(sem.sent, k)
+        return
+
+    me = plan[rank]
+    g.sync.dma_start(T.W[:, rank * WW:rank * WW + 128], T.w1[:]).then_inc(sem.loaded, 16)
+    g.scalar.dma_start(T.W[:, rank * WW + 128:(rank + 1) * WW], T.w2[:]).then_inc(sem.loaded, 16)
+    g.sync.wait_ge(sem.loaded, 32)
+    g.sync.dma_start(T.xs[:], T.x[:]).then_inc(sem.xl, 16)
+
+    g.wait_ge(sem.loaded, 32)
+    left = send(rank, [h for h, _ in me["helpers"]], sem.fed)
+    left += send(rank, [cores[t] for t in me["direct"]], sem["a%d" % rank])
+
+    due = [(-1.0, rank)]
+    count = {}
+    for s, p in enumerate(plan):
+        if rank in p["direct"]:
+            due.append((float(p["direct"].index(rank)), s))
+            count[s] = _bits(common_mask(cores[s], [cores[t] for t in p["direct"]]))
+        for k, (h, ts) in enumerate(p["helpers"]):
+            if rank in ts:
+                due.append((100.0 + ts.index(rank) + 0.25 * k, s))
+                count[s] = _bits(common_mask(h, [cores[t] for t in ts]))
+    order = [s for _, s in sorted(due)]
+    assert sorted(order) == list(range(N))
+    hp = [T["hp%d" % b] for b in range(BANKS)]
+
+    def mm1(i):
+        s = order[i]
+        if s == rank:
+            g.tensor.wait_ge(sem.loaded, 32)
+        else:
+            g.tensor.wait_ge(sem["a%d" % s], count[s])
+        g.tensor.matmul(hp[i % BANKS][:, 0:TK], T.W[:, s * WW:s * WW + 128], T.xs[:], True, True
+                        ).then_inc(sem["m%d" % i], 1)
+
+    def mm2(i):
+        s = order[i]
+        g.tensor.wait_ge(sem["r%d" % i], 1)
+        ins = g.tensor.matmul(T.yp[:, 0:TK], T.W[:, s * WW + 128:(s + 1) * WW], T.hs[:, i * TK:(i + 1) * TK],
+                              i == 0, i == N - 1)
+        if i == N - 1:
+            ins.then_inc(sem.yd, 1)
+
+    g.tensor.wait_ge(sem.xl, 16)
+    mm1(0)
+    for i in range(1, N):
+        mm1(i)
+        mm2(i - 1)
+    mm2(N - 1)
+
+    g.vector.memset(T.zero[:], 0.0).then_inc(sem.z, 1)
+    g.vector.wait_ge(sem.z, 1)
+    for i in range(N):
+        g.vector.wait_ge(sem["m%d" % i], 1)
+        g.vector.tensor_tensor(T.hs[:, i * TK:(i + 1) * TK], hp[i % BANKS][:, 0:TK], T.zero[:], AluOpType.max
+                               ).then_inc(sem["r%d" % i], 1)
+    g.vector.wait_ge(sem.yd, 1)
+    g.vector.tensor_copy(T.ys[:], T.yp[:, 0:TK]).then_inc(sem.yc, 1)
+
+    g.sync.wait_ge(sem.yc, 1)
+    g.sync.dma_start(T.y[:], T.ys[:]).then_inc(sem.stored, 16)
+    g.sync.wait_ge(sem.stored, 16)
+    g.wait_ge(sem.sent, left)

@@ -44,13 +44,12 @@ def _plan(cores, topo):
         far = ([c for c in port if topo.die(c) != topo.die(R)]
                + [c for c in mine if c not in port and topo.die(c) != topo.die(R)])
         direct, rest = ring[:DIRECT], ring[DIRECT:]
-        q = 2 * max(1, g // len(oth))
         rot = [(k + i) % len(oth) for k in range(len(oth))]
-        nx = [oth[k] for k in rot if (i + k) % q == 0]
-        fx = [oth[k] for k in rot if (i + k) % q != 0]
-        fill = len(nx) % PER
+        nx = [oth[k] for k in rot if (i + k) % 2 == 0]
+        fx = [oth[k] for k in rot if (i + k) % 2 != 0]
+        half = len(rest) // 2
         helpers = []
-        for lst, cs in ((fx + rest[fill:], far), (nx + rest[:fill], near)):
+        for lst, cs in ((fx + rest[half:], far), (nx + rest[:half], near)):
             for j in range(0, len(lst), PER):
                 helpers.append((cs[j // PER], lst[j:j + PER]))
         for h, ts in helpers:

@@ -4,7 +4,8 @@ from concourse.mybir import AluOpType
 N = 12
 TK = 64
 WW = 256
-BANKS = 4
+LAG = 6
+BANKS = LAG + 1
 DIRECT = 3
 PER = 2
 
@@ -137,11 +138,11 @@ def rank_program(g, core, T, topo):
             ins.then_inc(sem.yd, 1)
 
     g.tensor.wait_ge(sem.xl, 16)
-    mm1(0)
-    for i in range(1, N):
-        mm1(i)
-        mm2(i - 1)
-    mm2(N - 1)
+    for i in range(N + LAG):
+        if i < N:
+            mm1(i)
+        if i >= LAG:
+            mm2(i - LAG)
 
     g.vector.memset(T.zero[:], 0.0).then_inc(sem.z, 1)
     g.vector.wait_ge(sem.z, 1)

@@ -4,8 +4,7 @@ from concourse.mybir import AluOpType
 N = 12
 TK = 64
 WW = 256
-LAG = 6
-BANKS = LAG + 1
+BANKS = 7
 DIRECT = 3
 PER = 2
 
@@ -20,8 +19,9 @@ SCRATCH = {
 for _b in range(BANKS):
     SCRATCH["hp%d" % _b] = ("psum", [128, 512], "float32")
 
-SEMAPHORES = (["loaded", "xl", "fed", "sent", "z", "yd", "yc", "stored"]
+SEMAPHORES = (["l1", "l2", "xl", "fed1", "fed2", "sent", "z", "yd", "yc", "stored"]
               + ["a%d" % _i for _i in range(N)]
+              + ["b%d" % _i for _i in range(N)]
               + ["m%d" % _i for _i in range(N)]
               + ["r%d" % _i for _i in range(N)])
 
@@ -70,20 +70,19 @@ def rank_program(g, core, T, topo):
     plan = _CACHE["plan"]
     sem = T.sem
 
-    def slot(s):
-        return T.W[:, s * WW:(s + 1) * WW]
-
     def common_mask(src, dsts):
         m = topo.mask(src, dsts[0])
         for d in dsts[1:]:
             m &= topo.mask(src, d)
         return m
 
-    def send(s, dsts, rsem):
+    def send(s, lo, hi, dsts, rsem):
         m = common_mask(core, dsts)
         ids = [DstId(rid=topo.addr(d)[0], pnc=topo.addr(d)[1]) for d in dsts]
-        g.remote_dma_fused([RemoteDMATransfer(dst_ids=ids, dma_engine_mask=m, remote_sem=rsem, srcs=[slot(s)],
-                                              dsts=[slot(s) for _ in dsts], alu_op=0)], local_sem=sem.sent)
+        g.remote_dma_fused([RemoteDMATransfer(dst_ids=ids, dma_engine_mask=m, remote_sem=rsem,
+                                              srcs=[T.W[:, s * WW + lo:s * WW + hi]],
+                                              dsts=[T.W[:, s * WW + lo:s * WW + hi] for _ in dsts], alu_op=0)],
+                           local_sem=sem.sent)
         return _bits(m)
 
     rank = T.rank_of(core)
@@ -91,23 +90,34 @@ def rank_program(g, core, T, topo):
         for s, p in enumerate(plan):
             for h, ts in p["helpers"]:
                 if h == core:
-                    g.wait_ge(sem.fed, _bits(common_mask(cores[s], [c for c, _ in p["helpers"]])))
-                    k = send(s, [cores[t] for t in ts], sem["a%d" % s])
+                    fed = _bits(common_mask(cores[s], [c for c, _ in p["helpers"]]))
+                    g.wait_ge(sem.fed1, fed)
+                    k = send(s, 0, 128, [cores[t] for t in ts], sem["a%d" % s])
+                    g.wait_ge(sem.fed2, fed)
+                    k += send(s, 128, WW, [cores[t] for t in ts], sem["b%d" % s])
                     g.wait_ge(sem.sent, k)
         return
 
     me = plan[rank]
-    g.sync.dma_start(T.W[:, rank * WW:rank * WW + 128], T.w1[:]).then_inc(sem.loaded, 16)
-    g.scalar.dma_start(T.W[:, rank * WW + 128:(rank + 1) * WW], T.w2[:]).then_inc(sem.loaded, 16)
-    g.sync.wait_ge(sem.loaded, 32)
+    c0 = rank * WW
+    g.sync.dma_start(T.W[0:64, c0:c0 + 128], T.w1[0:64, :]).then_inc(sem.l1, 16)
+    g.scalar.dma_start(T.W[64:128, c0:c0 + 128], T.w1[64:128, :]).then_inc(sem.l1, 16)
+    g.sync.dma_start(T.W[0:64, c0 + 128:c0 + WW], T.w2[0:64, :]).then_inc(sem.l2, 16)
+    g.scalar.dma_start(T.W[64:128, c0 + 128:c0 + WW], T.w2[64:128, :]).then_inc(sem.l2, 16)
+    g.sync.wait_ge(sem.l1, 32)
+    g.sync.wait_ge(sem.l2, 32)
     g.sync.dma_start(T.xs[:], T.x[:]).then_inc(sem.xl, 16)
 
-    g.wait_ge(sem.loaded, 32)
-    left = send(rank, [h for h, _ in me["helpers"]], sem.fed)
-    left += send(rank, [cores[t] for t in me["direct"]], sem["a%d" % rank])
+    mates = [h for h, _ in me["helpers"]]
+    g.wait_ge(sem.l1, 32)
+    left = send(rank, 0, 128, mates, sem.fed1)
+    g.wait_ge(sem.l2, 32)
+    left += send(rank, 128, WW, mates, sem.fed2)
+    left += send(rank, 0, WW, [cores[t] for t in me["direct"]], sem["a%d" % rank])
 
     due = [(-1.0, rank)]
     count = {}
+    halves = set()
     for s, p in enumerate(plan):
         if rank in p["direct"]:
             due.append((float(p["direct"].index(rank)), s))
@@ -116,33 +126,31 @@ def rank_program(g, core, T, topo):
             if rank in ts:
                 due.append((100.0 + ts.index(rank) + 0.25 * k, s))
                 count[s] = _bits(common_mask(h, [cores[t] for t in ts]))
+                halves.add(s)
     order = [s for _, s in sorted(due)]
     assert sorted(order) == list(range(N))
     hp = [T["hp%d" % b] for b in range(BANKS)]
 
-    def mm1(i):
-        s = order[i]
+    g.tensor.wait_ge(sem.xl, 16)
+    for i, s in enumerate(order):
         if s == rank:
-            g.tensor.wait_ge(sem.loaded, 32)
+            g.tensor.wait_ge(sem.l1, 32)
         else:
             g.tensor.wait_ge(sem["a%d" % s], count[s])
+        if i >= BANKS:
+            g.tensor.wait_ge(sem["r%d" % (i - BANKS)], 1)
         g.tensor.matmul(hp[i % BANKS][:, 0:TK], T.W[:, s * WW:s * WW + 128], T.xs[:], True, True
                         ).then_inc(sem["m%d" % i], 1)
-
-    def mm2(i):
-        s = order[i]
+    for i, s in enumerate(order):
+        if s == rank:
+            g.tensor.wait_ge(sem.l2, 32)
+        elif s in halves:
+            g.tensor.wait_ge(sem["b%d" % s], count[s])
         g.tensor.wait_ge(sem["r%d" % i], 1)
         ins = g.tensor.matmul(T.yp[:, 0:TK], T.W[:, s * WW + 128:(s + 1) * WW], T.hs[:, i * TK:(i + 1) * TK],
                               i == 0, i == N - 1)
         if i == N - 1:
             ins.then_inc(sem.yd, 1)
-
-    g.tensor.wait_ge(sem.xl, 16)
-    for i in range(N + LAG):
-        if i < N:
-            mm1(i)
-        if i >= LAG:
-            mm2(i - LAG)
 
     g.vector.memset(T.zero[:], 0.0).then_inc(sem.z, 1)
     g.vector.wait_ge(sem.z, 1)

from concourse.bass import DstId, RemoteDMATransfer
from concourse.mybir import AluOpType

N = 12
TK = 64
WW = 256
BANKS = 7
DIRECT = 3
PER = 2

SCRATCH = {
    "W": ("sbuf", [128, N * WW], "bfloat16"),
    "xs": ("sbuf", [128, TK], "bfloat16"),
    "hs": ("sbuf", [128, N * TK], "bfloat16"),
    "zero": ("sbuf", [128, TK], "float32"),
    "ys": ("sbuf", [128, TK], "bfloat16"),
    "yp": ("psum", [128, 512], "float32"),
}
for _b in range(BANKS):
    SCRATCH["hp%d" % _b] = ("psum", [128, 512], "float32")

SEMAPHORES = (["l1", "l2", "xl", "fed1", "fed2", "sent", "z", "yd", "yc", "stored"]
              + ["a%d" % _i for _i in range(N)]
              + ["b%d" % _i for _i in range(N)]
              + ["m%d" % _i for _i in range(N)]
              + ["r%d" % _i for _i in range(N)])

_CACHE = {}


def _plan(cores, topo):
    n = len(cores)
    chips = [topo.chip(c) for c in cores]
    every = range(topo.CHIPS * topo.CORES_PER_CHIP)
    out = []
    for s, R in enumerate(cores):
        grp = [t for t in range(n) if t == s or topo.same_plane(chips[s], chips[t])]
        oth = [t for t in range(n) if t not in grp]
        i, g = grp.index(s), len(grp)
        ring = [grp[(i + k) % g] for k in range(1, g)]
        mine = [c for c in every if topo.chip(c) == chips[s] and c != R]
        port = [c for c in mine if all(topo.may_write(c, cores[t]) for t in oth)]
        near = ([c for c in port if topo.die(c) == topo.die(R)]
                + [c for c in mine if c not in port and topo.die(c) == topo.die(R)])
        far = ([c for c in port if topo.die(c) != topo.die(R)]
               + [c for c in mine if c not in port and topo.die(c) != topo.die(R)])
        direct, rest = ring[:DIRECT], ring[DIRECT:]
        rot = [(k + i) % len(oth) for k in range(len(oth))]
        nx = [oth[k] for k in rot if (i + k) % 2 == 0]
        fx = [oth[k] for k in rot if (i + k) % 2 != 0]
        half = len(rest) // 2
        helpers = []
        for lst, cs in ((fx + rest[half:], far), (nx + rest[:half], near)):
            for j in range(0, len(lst), PER):
                helpers.append((cs[j // PER], lst[j:j + PER]))
        for h, ts in helpers:
            assert all(topo.may_write(h, cores[t]) for t in ts)
        out.append({"direct": direct, "helpers": helpers})
    return out


def _bits(m):
    return bin(m).count("1")


def rank_program(g, core, T, topo):
    cores = list(T.cores)
    if "plan" not in _CACHE:
        _CACHE["plan"] = _plan(cores, topo)
    plan = _CACHE["plan"]
    sem = T.sem

    def common_mask(src, dsts):
        m = topo.mask(src, dsts[0])
        for d in dsts[1:]:
            m &= topo.mask(src, d)
        return m

    def send(s, lo, hi, dsts, rsem):
        m = common_mask(core, dsts)
        ids = [DstId(rid=topo.addr(d)[0], pnc=topo.addr(d)[1]) for d in dsts]
        g.remote_dma_fused([RemoteDMATransfer(dst_ids=ids, dma_engine_mask=m, remote_sem=rsem,
                                              srcs=[T.W[:, s * WW + lo:s * WW + hi]],
                                              dsts=[T.W[:, s * WW + lo:s * WW + hi] for _ in dsts], alu_op=0)],
                           local_sem=sem.sent)
        return _bits(m)

    rank = T.rank_of(core)
    if rank is None:
        for s, p in enumerate(plan):
            for h, ts in p["helpers"]:
                if h == core:
                    fed = _bits(common_mask(cores[s], [c for c, _ in p["helpers"]]))
                    g.wait_ge(sem.fed1, fed)
                    k = send(s, 0, 128, [cores[t] for t in ts], sem["a%d" % s])
                    g.wait_ge(sem.fed2, fed)
                    k += send(s, 128, WW, [cores[t] for t in ts], sem["b%d" % s])
                    g.wait_ge(sem.sent, k)
        return

    me = plan[rank]
    c0 = rank * WW
    g.sync.dma_start(T.W[0:64, c0:c0 + 128], T.w1[0:64, :]).then_inc(sem.l1, 16)
    g.scalar.dma_start(T.W[64:128, c0:c0 + 128], T.w1[64:128, :]).then_inc(sem.l1, 16)
    g.sync.dma_start(T.W[0:64, c0 + 128:c0 + WW], T.w2[0:64, :]).then_inc(sem.l2, 16)
    g.scalar.dma_start(T.W[64:128, c0 + 128:c0 + WW], T.w2[64:128, :]).then_inc(sem.l2, 16)
    g.sync.wait_ge(sem.l1, 32)
    g.sync.wait_ge(sem.l2, 32)
    g.sync.dma_start(T.xs[:], T.x[:]).then_inc(sem.xl, 16)

    mates = [h for h, _ in me["helpers"]]
    g.wait_ge(sem.l1, 32)
    left = send(rank, 0, 128, mates, sem.fed1)
    g.wait_ge(sem.l2, 32)
    left += send(rank, 128, WW, mates, sem.fed2)
    left += send(rank, 0, WW, [cores[t] for t in me["direct"]], sem["a%d" % rank])

    due = [(-1.0, rank)]
    count = {}
    halves = set()
    for s, p in enumerate(plan):
        if rank in p["direct"]:
            due.append((float(p["direct"].index(rank)), s))
            count[s] = _bits(common_mask(cores[s], [cores[t] for t in p["direct"]]))
        for k, (h, ts) in enumerate(p["helpers"]):
            if rank in ts:
                due.append((100.0 + ts.index(rank) + 0.25 * k, s))
                count[s] = _bits(common_mask(h, [cores[t] for t in ts]))
                halves.add(s)
    order = [s for _, s in sorted(due)]
    assert sorted(order) == list(range(N))
    hp = [T["hp%d" % b] for b in range(BANKS)]

    g.tensor.wait_ge(sem.xl, 16)
    for i, s in enumerate(order):
        if s == rank:
            g.tensor.wait_ge(sem.l1, 32)
        else:
            g.tensor.wait_ge(sem["a%d" % s], count[s])
        if i >= BANKS:
            g.tensor.wait_ge(sem["r%d" % (i - BANKS)], 1)
        g.tensor.matmul(hp[i % BANKS][:, 0:TK], T.W[:, s * WW:s * WW + 128], T.xs[:], True, True
                        ).then_inc(sem["m%d" % i], 1)
    for i, s in enumerate(order):
        if s == rank:
            g.tensor.wait_ge(sem.l2, 32)
        elif s in halves:
            g.tensor.wait_ge(sem["b%d" % s], count[s])
        g.tensor.wait_ge(sem["r%d" % i], 1)
        ins = g.tensor.matmul(T.yp[:, 0:TK], T.W[:, s * WW + 128:(s + 1) * WW], T.hs[:, i * TK:(i + 1) * TK],
                              i == 0, i == N - 1)
        if i == N - 1:
            ins.then_inc(sem.yd, 1)

    g.vector.memset(T.zero[:], 0.0).then_inc(sem.z, 1)
    g.vector.wait_ge(sem.z, 1)
    for i in range(N):
        g.vector.wait_ge(sem["m%d" % i], 1)
        g.vector.tensor_tensor(T.hs[:, i * TK:(i + 1) * TK], hp[i % BANKS][:, 0:TK], T.zero[:], AluOpType.max
                               ).then_inc(sem["r%d" % i], 1)
    g.vector.wait_ge(sem.yd, 1)
    g.vector.tensor_copy(T.ys[:], T.yp[:, 0:TK]).then_inc(sem.yc, 1)

    g.sync.wait_ge(sem.yc, 1)
    g.sync.dma_start(T.y[:], T.ys[:]).then_inc(sem.stored, 16)
    g.sync.wait_ge(sem.stored, 16)
    g.wait_ge(sem.sent, left)
